import numpy as np, ml_dtypes
CORES = [1,5,17,21,33,37,49,53]
N = 8
BF = ml_dtypes.bfloat16
def gentries(a):
    return np.ascontiguousarray(a.reshape(8, 16, -1).transpose(0, 2, 1)).reshape(8, -1)
def gtable(e):
    e = np.asarray(e); return np.ascontiguousarray(e.reshape(8, -1, 16).transpose(0, 2, 1)).reshape(128, -1).astype(np.int32)
W, I, J, A, B, P, RO = 4096, 1536, 2048, 16, 8, 64, 5
def column(i, j):
    return ((((2 * i + 1) * (2 * j + 1)) >> 5) + 37 * i + j) & (W - 1)
def sized(rng, n, lo, hi, noise):
    b = np.exp2(lo + (hi - lo) * rng.random((N, 8, 1, n), dtype=np.float32))
    return (b * np.exp2(noise * (2 * rng.random((N, 8, 16, n), dtype=np.float32) - 1))).astype(np.int64)
def parts(rng):
    v = np.minimum(np.maximum(sized(rng, W, 2.6, 6.8, 0.5), 1), 127)
    rl = rng.integers(0, J, (N, 8, 16, I)); cl = rng.integers(0, I, (N, 8, 16, J))
    i = rng.integers(0, I, (N, 8, P)); j = rng.integers(0, J, (N, 8, P))
    return v, rl, cl, i, j, np.minimum(sized(rng, P, 1.0, 6.0, 0.5), 127)
def pack(v, rl, cl, i, j, z):
    return {"fig": np.ascontiguousarray(v.reshape(N, 128, W)).astype(np.float32).astype(BF), "rmate": np.ascontiguousarray(rl.reshape(N, 128, I)).astype(np.int32), "cmate": np.ascontiguousarray(cl.reshape(N, 128, J)).astype(np.int32),
            "prow": np.stack([gtable(a) for a in i]), "pcol": np.stack([gtable(a) for a in j]), "need": np.ascontiguousarray(z.reshape(N, 128, P)).astype(np.float32).astype(BF)}
def some(rng, good, free):
    n = np.flatnonzero(good & free)
    if len(n) == 0: n = np.flatnonzero(free)
    return n[rng.integers(0, len(n), 128)]
def fill(rng, v, rl, cl, i, j, z, g):
    v[:, g] = 40 + np.argsort(rng.random((N, 16, W)), axis=1); z[:, g] = 0
    seen = np.zeros((N, W), bool); rows = np.zeros((N, I), bool); cols = np.zeros((N, J), bool); ai = np.arange(I); aj = np.arange(J)
    for q in range(N):
        i[q, g] = rng.permutation(I)[:P]; j[q, g] = rng.permutation(J)[:P]; rows[q, i[q, g]] = True; cols[q, j[q, g]] = True
    x = np.array(i[:, g]); y = np.array(j[:, g])
    for t in range(RO):
        if t == RO - 1: rows[:] = False; cols[:] = False
        nx = np.zeros_like(x); ny = np.zeros_like(y)
        for q in range(N):
            to = (q + 1 + t % 3) % N
            for k in range(P):
                a, b = int(x[q, k]), int(y[q, k])
                u = some(rng, ~seen[q][column(a, aj)], ~cols[to]); w = some(rng, ~seen[q][column(ai, b)], ~rows[to])
                c = np.stack([column(a, u), column(w, b), column(w, u)])
                n = int(np.argmax(~seen[q][c[2]] & (c[0] != c[1]) & (c[0] != c[2]) & (c[1] != c[2])))
                seen[q, c[:, n]] = True; cols[to, u[n]] = True; rows[to, w[n]] = True
                rl[q, g, :, a] = u[n]; cl[q, g, :, b] = w[n]; nx[to, k] = w[n]; ny[to, k] = u[n]
        x, y = nx, ny
def setup_inputs(rng):
    return pack(*parts(rng))
def setup_inputs_ties(rng):
    v, rl, cl, i, j, z = parts(rng)
    v = rng.choice(np.array([8, 16, 32, 64]), (N, 8, 1, W)) + np.zeros((1, 1, 16, 1), np.int64)
    low = (rng.random((N, 8, 1, W)) < 0.3) & (np.arange(16)[:, None] == rng.integers(0, 16, (N, 8, 1, W)))
    z = rng.choice(np.array([0, 1, 8, 9, 16, 32, 33, 64, 65]), (N, 8, 1, P)) + np.zeros((1, 1, 16, 1), np.int64)
    v = v - low; fill(rng, v, rl, cl, i, j, z, 3)
    return pack(v, rl, cl, i, j, z)
def setup_inputs_none(rng):
    v, rl, cl, i, j, z = parts(rng)
    h = int(rng.integers(0, 8)); z[int(rng.integers(0, N))] = 0; z[:, h] = 127; v[:, h] = np.minimum(v[:, h], 126)
    for g, a, b in (((h + 1) % 8, A - 1, B - 1), ((h + 2) % 8, 0, 0)):
        v[:, g] = np.minimum(v[:, g], 10); z[:, g] = rng.integers(20, 30, (N, 16, P))
        for q in range(N):
            for k in range(8):
                x, y = int(i[q, g, k]), int(j[q, g, k]); u, w = int(rl[q, g, a, x]), int(cl[q, g, b, y])
                for c in (column(x, u), column(w, y), column(w, u)): v[q, g, :, c] = 127
    return pack(v, rl, cl, i, j, z)
def setup_inputs_alike(rng):
    v, rl, cl, i, j, z = parts(rng); z = z // 4
    i[:, [0, 4]] = i[:, [0, 4], :1]; j[:, [0, 4]] = j[:, [0, 4], :1]; z[:, [0, 4]] = z[:, [0, 4], :, :1]
    rl[:, [1, 5]] = rng.choice(np.array([0, 5, J - 1]), (N, 2, 16, I)); cl[:, [1, 5]] = rng.choice(np.array([0, 7, I - 1]), (N, 2, 16, J))
    i[:, 2] = rng.choice(np.array([0, 1, I // 2, I - 1]), (N, P)); j[:, 2] = rng.choice(np.array([0, 1, J // 2, J - 1]), (N, P))
    rl[:, 6] = rl[:, 6, :1]; cl[:, 6] = cl[:, 6, :1]
    for q in range(N):
        rl[q, 7, 0, i[q, 7]] = j[q, 7]; cl[q, 7, 0, j[q, 7]] = i[q, 7]
        cl[q, 4, :, int(j[q, 4, 0])] = int(i[q, 4, 0])
    z[:, 4] = 0
    rl[:, 3] = np.where(rng.random((N, 16, I)) < 0.5, rng.choice(np.array([0, J - 1]), (N, 16, I)), rl[:, 3])
    cl[:, 3] = np.where(rng.random((N, 16, J)) < 0.5, rng.choice(np.array([0, I - 1]), (N, 16, J)), cl[:, 3])
    i[:, 3] = np.where(rng.random((N, P)) < 0.5, rng.choice(np.array([0, I - 1]), (N, P)), i[:, 3])
    j[:, 3] = np.where(rng.random((N, P)) < 0.5, rng.choice(np.array([0, J - 1]), (N, P)), j[:, 3])
    return pack(v, rl, cl, i, j, z)
def setup_inputs_late(rng):
    v, rl, cl, i, j, z = parts(rng); z = z // 4
    for g in range(8):
        s = rng.permutation(16)
        for q in range(N):
            a, b = int(s[q % 2]), int(s[1 - q % 2])
            v[q, g, a] = np.minimum(v[q, g, a], 12); z[q, g, a] = rng.integers(13, 30, P); z[q, g, b] = np.minimum(z[q, g, b], 6)
    return pack(v, rl, cl, i, j, z)
def setup_inputs_spread(rng):
    v, rl, cl, i, j, z = parts(rng)
    v = np.minimum(np.maximum(sized(rng, W, 0.0, 7.3, 0.3), 1), 127)
    z = np.minimum(sized(rng, P, -1.0, 7.2, 0.2), 127)
    v[:, 2] = rng.integers(123, 128, (N, 16, W)); z[:, 2] = np.minimum(z[:, 2], 60)
    v[:, 5] = np.where(rng.random((N, 1, W)) < 0.5, 127, 1); z[:, 5] = 127
    return pack(v, rl, cl, i, j, z)
def check_inputs(d):
    bad = []
    for k, lo, hi in (("fig", 1, 127), ("rmate", 0, J - 1), ("cmate", 0, I - 1), ("prow", 0, I - 1), ("pcol", 0, J - 1), ("need", 0, 127)):
        v = np.asarray(d[k]).astype(np.float64)
        if not (np.all(v >= lo) and np.all(v <= hi) and np.all(v == np.floor(v))): bad.append("range of " + k)
    return bad
def look(h, c, z):
    m = c.shape[1]; v = np.take_along_axis(h, c.reshape(8, 1, m * P), 2).reshape(8, 16, m, P)
    return np.all(np.abs(v) >= z[:, :, None, :], axis=1), np.sum(np.maximum(v, 0), axis=1)
def reference(fig, rmate, cmate, prow, pcol, need):
    h = fig.astype(np.float32).astype(np.int32).reshape(N, 8, 16, W); z = need.astype(np.float32).astype(np.int32).reshape(N, 8, 16, P)
    rm = rmate.astype(np.int64).reshape(N, 8, 16, I); cm = cmate.astype(np.int64).reshape(N, 8, 16, J)
    i = np.stack([gentries(a) for a in prow]).astype(np.int64); j = np.stack([gentries(a) for a in pcol]).astype(np.int64)
    cost = np.zeros((N, 8, RO, P), np.float32); gi = np.arange(8)[:, None] + np.zeros((1, P), np.int64)
    for t in range(RO):
        ra = A * (t % (16 // A)); rb = B * (t % (16 // B)); sh = 1 + t % 3
        ni, nj, nz = [None] * N, [None] * N, [None] * N
        for q in range(N):
            x, y = i[q], j[q]
            jm = np.take_along_axis(rm[q][:, ra:ra + A], x[:, None, :], 2)
            im = np.take_along_axis(cm[q][:, rb:rb + B], y[:, None, :], 2)
            ok1, c1 = look(h[q], column(x[:, None, :], jm), z[q]); ok2, c2 = look(h[q], column(im, y[:, None, :]), z[q])
            ok3, c3 = look(h[q], column(im[:, None, :, :], jm[:, :, None, :]).reshape(8, A * B, P), z[q])
            ok = (ok1[:, :, None, :] & ok2[:, None, :, :]).reshape(8, A * B, P) & ok3
            total = (c1[:, :, None, :] + c2[:, None, :, :]).reshape(8, A * B, P) + c3
            total = np.where(ok, total, 2 ** 20)
            best = np.argmin(total, axis=1); good = np.any(ok, axis=1)
            cost[q, :, t] = np.where(good, np.take_along_axis(total, best[:, None, :], 1)[:, 0], -1)
            u = np.take_along_axis(jm, (best // B)[:, None, :], 1)[:, 0]; w = np.take_along_axis(im, (best % B)[:, None, :], 1)[:, 0]
            far = column(w, u); hit = np.zeros((8, W), bool)
            for c in (column(x, u), column(w, y), far): hit[gi[good], c[good]] = True
            size = np.abs(h[q]); fresh = np.take_along_axis(size, far[:, None, :], 2) >> 1
            h[q] = np.where(hit[:, None, :], -size, h[q])
            to = (q + sh) % N
            ni[to] = np.where(good, w, x); nj[to] = np.where(good, u, y); nz[to] = np.where(good[:, None, :], fresh, z[q])
        i = np.stack(ni); j = np.stack(nj); z = np.stack(nz)
    yp = np.stack([gtable(np.concatenate([i[q], j[q]], axis=1)) for q in range(N)])
    return {"yf": h.reshape(N, 128, W).astype(np.float32).astype(BF), "yp": yp.astype(np.float32), "yz": z.reshape(N, 128, P).astype(np.float32).astype(BF), "yc": cost.reshape(N, 8, RO * P)}

@@ -1,0 +1,352 @@
+from concourse.mybir import AluOpType as Op, AxisListType, ActivationFunctionType as Act
+
+W, P, RO = 4096, 64, 5
+ROT = 315
+BAD = float(1 << 20)
+BIG = float(1 << 27)
+OUT = 16384.0
+SCRATCH = {}
+
+
+def _bufs(dtype, text, where="sbuf"):
+    for item in text.split(","):
+        f = item.split()
+        SCRATCH[f[0]] = (where, [int(f[2]) if len(f) > 2 else 128, int(f[1])], dtype)
+
+
+_bufs("bfloat16", "GF2 512, GP2 512, C2f 64 64, EXf 128 64, FA 4160, PP 4160, NA 4096, ND 64, MM 384, NS 320, NR 1024, GF 9216, GP 9216, AB 768, MN 768, ZER 64, YZo 64")
+_bufs("bfloat16", "TBf 128 8, B01 64 8, E8 128 8, E8o 128 8, LIDX 128 2, IDXR 512 2, INDF 64, INDP 64, IND1 64, DIAG 192, RS16 192, RS64 768, ONE 128 2, XPRE 256 1, JPRE 160 2, MPRE 192 1")
+_bufs("int32", "RM 1536, CM 2048, PR 8, PI 1, CI 768, TI 256, DI 12, GPi 1, SPi 1, MG 128, MS 192, M7 128, M1 128 8, MH 128 64, M8 64, C63 768, Pc 608, Pi 608, KM 640 8, T32 128 8, PF 192, FI 192, YI 320 8")
+_bufs("uint16", "LL 48, LS 40, OF 608, TNu 4, TS 12")
+_bufs("float16", "C2p 64 64, EXp 128 64, IJ 768, IS 640, IJD 128, BLK 128, SEL 2048, DUP 512, M2S 256, TMP 512, ID 128, I2 128, I2h 256, EI 128, EJ 128, SELW 128, SELJ 128, TRI 256, Xf 64, UAW 128, VD 192")
+_bufs("float32", "PRf 8, GPf 1, SPf 1, PIf 1, SPQ 16, SPm 2, IDf 128, cX 1, cW 1, cJ 1, ownA 1, ownB 1, ownT 1, RS2 128 8, DUM 12, Yp 64, YM 128, Y2 32, S1 8, LD 128, LSc 128, UWs 128, SL 192, TN 4, DU 12, DV 12, DW 12, YT 320 8, YC 320 8, YPo 8")
+_bufs("float32", "XB0 512, XB1 512, JI 512, MB 512, KT 512, TAB 512, UW 512, KEY 512", "psum")
+SCRATCH["KEY"] = ("psum", [128, 8, 64], "float32")
+SEMAPHORES = ["sV", "sS", "sT", "sP", "ls", "out", "gd", "gd2"] + ["ld%d" % k for k in range(7)] + ["%s%d" % (m, t) for m in "lin" for t in range(1, RO + 1)]
+
+
+def rank_program(g, core, T, topo):
+    rank = T.rank_of(core)
+    if rank is None:
+        return
+    n_ranks = len(T.cores)
+    QS = {"V": g.vector, "S": g.scalar, "T": g.tensor, "P": g, "D": g.sync}
+    cnt = {q: 0 for q in "VSTP"}
+    known = {q: {} for q in QS}
+    snaps = {}
+    hist = {}
+
+    def v(name, lo=0, hi=None, st=1, r=None):
+        hi = SCRATCH[name][1][1] if hi is None else hi
+        return T[name][0:(r or SCRATCH[name][1][0]), lo:hi:st], [(name, lo, hi, st)]
+    def w(name, lo, n, st=1): return v(name, lo, lo + n * st, st)
+    def ix(name, hi, lst): return T[name][:, 0:hi].indirect(lst[0]), [(name, 0, hi, 1)] + lst[1]
+    def key(ap): return ap, [("KEY", 0, 512, 1)]
+    def ext(ap, name=None): return ap, [(name, 0, 1, 1)] if name else []
+
+    def wait(q, ev, n):
+        if known[q].get(ev, 0) < n:
+            QS[q].wait_ge(T.sem["s" + ev if ev in cnt else ev], n)
+            known[q][ev] = n
+            for e2, n2 in snaps.get((ev, n), {}).items(): known[q][e2] = max(known[q].get(e2, 0), n2)
+
+    def order(q, rd, wr, ev, n):
+        need = {}
+        acc = [(x, False) for o in rd for x in o[1]] + [(x, True) for x in wr[1]]
+        for (name, lo, hi, st), write in acc:
+            bank = SCRATCH[name][0] == "psum" if name in SCRATCH else False
+            for a in hist.get(name, []):
+                apart = a[1] <= lo or hi <= a[0] or (a[2] == st > 1 and (a[0] - lo) % st)
+                if bank and a[3] != q: apart = False
+                elif not (write or a[5]) or (q == a[3] == "T"): continue
+                if not apart: need[a[3]] = max(need.get(a[3], 0), a[4])
+        for e, c in sorted(need.items(), key=lambda x: (x[0] == q, x[0])): wait(q, e, c)
+        snaps[(ev, n)] = dict(known[q])
+        for (name, lo, hi, st), write in acc:
+            bank = SCRATCH[name][0] == "psum" if name in SCRATCH else False
+            hist[name] = [a for a in hist.get(name, []) if not ((bank and a[3] != q) or (lo <= a[0] and a[1] <= hi and a[2] % st == 0 and (a[0] - lo) % st == 0 and (write or (a[3] == ev and not a[5]))))]
+            hist[name].append([lo, hi, st, ev, n, write])
+
+    def do(q, fn, out, ins, args, **kw):
+        order(q, ins, out, q, cnt[q] + 1)
+        cnt[q] += 1
+        fn(out[0], *args, **kw).then_inc(T.sem["s" + q], 1)
+
+    def dma(q, ev, n, out, in_, **kw):
+        order(q, [in_], out, ev, n)
+        QS[q].dma_start(out[0], in_[0], **kw).then_inc(T.sem[ev], 16)
+
+    def vc(out, a): do("V", g.vector.tensor_copy, out, [a], (a[0],))
+    def tt(out, a, b, op): do("V", g.vector.tensor_tensor, out, [a, b], (a[0], b[0], op))
+    def ts(out, a, s1, op0, s2=None, op1=None):
+        col = isinstance(s1, tuple)
+        do("V", g.vector.tensor_scalar, out, [a, s1] if col else [a], (a[0], s1[0] if col else s1, s2, op0) + ((op1,) if op1 else ()))
+    def scan(out, d0, d1, op0, op1): do("V", g.vector.tensor_tensor_scan, out, [d0, d1], (d0[0], d1[0], 0.0, op0, op1))
+    def act(out, a, f=Act.Identity, bias=0.0, scale=1.0):
+        col = isinstance(bias, tuple)
+        do("S", g.scalar.activation, out, [a, bias] if col else [a], (a[0], f), bias=bias[0] if col else bias, scale=scale)
+    def mm(out, l, r, st, sp): do("T", g.tensor.matmul, out, [l, r], (l[0], r[0], st, sp))
+    def fill(out, c): do("V", g.vector.memset, out, [], (c,))
+    def iota(name, pattern, base, cm, **kw): do("P", g.iota, v(name), [], (pattern, base, cm), **kw)
+
+    sent = [0]
+
+    def send(what, t, out, in_):
+        dst = T.cores[(rank + 1 + t % 3) % n_ranks]
+        eng = topo.engines(core, dst)[:8]
+        sent[0] += len(eng)
+        order("P", [in_], ext(None), "ls", sent[0])
+        rid, pid, _ = topo.addr(dst)
+        g.remote_dma(out[0], in_[0], T.sem["%s%d" % (what, t + 1)], T.sem.ls, pid, rid, sum(1 << e for e in eng))
+
+    def landed(what, t, name, n):
+        src = T.cores[(rank - 1 - (t - 1) % 3) % n_ranks]
+        hist.setdefault(name, []).append([n * t, n * t + n, 1, "%s%d" % (what, t), len(topo.engines(src, core)[:8]), True])
+
+    dma("D", "ld0", 16, w("PR", 0, 4), ext(T.pcol[:]))
+    dma("D", "ld1", 16, w("PR", 4, 4), ext(T.prow[:]))
+    dma("S", "ld4", 16, v("RM"), ext(T.rmate[:]))
+    dma("D", "ld3", 16, v("CM"), ext(T.cmate[:]))
+    dma("D", "ld2", 16, v("ND"), ext(T.need[:]))
+    dma("D", "ld5", 16, v("FA", ROT, W), ext(T.fig[:, 0:W - ROT]))
+    dma("D", "ld6", 16, v("FA", 0, ROT), ext(T.fig[:, W - ROT:W]))
+
+    iota("PI", [[0, 1]], 0, 1)
+    iota("CI", [[1, 768]], 0, 0)
+    iota("IDXR", [[0, 8], [1, 8], [8, 8]], 0, 64, allow_small_or_imprecise_dtypes=True)
+    iota("TI", [[-16, 4], [1, 64]], 0, 0)
+    iota("DI", [[0, 3], [16, 4]], W - 2048, 0)
+    for name, c in (("ONE", 1.0), ("XPRE", 17.0), ("JPRE", 1.0), ("MPRE", -2048.0), ("ZER", 0.0)): fill(v(name), c)
+    fill(v("JPRE", 0, 64, 1, 1), 16.0)
+    fill(v("JPRE", 64, 160, 1, 1), 592.0)
+    c128, SP, GP_, PI = v("CI", 0, 128), v("SPf"), v("GPf"), v("PIf")
+    ts(v("SPi"), v("PI"), 15, Op.bitwise_and)
+    ts(v("GPi"), v("PI"), 4, Op.logical_shift_right)
+    ts(v("MG"), c128, 4, Op.logical_shift_right)
+    ts(v("MS"), v("CI", 0, 192), 15, Op.bitwise_and)
+    vc(SP, v("SPi")); vc(GP_, v("GPi")); vc(PI, v("PI"))
+    ts(v("BLK"), v("MG"), GP_, Op.is_equal)
+    ts(v("SPQ"), v("CI", 0, 16), SP, Op.is_equal, 2.0, Op.mult)
+    for s in range(8): ts(w("SEL", 128 * s, 128), v("BLK"), w("SPQ", s, 1), Op.mult)
+    ts(v("DIAG"), v("MS"), SP, Op.is_equal)
+    vc(w("LL", 0, 8), v("PR"))
+    vc(v("PRf"), v("PR"))
+    for q in range(8): ts(w("IJD", 16 * q, 16), w("DIAG", 0, 16), w("PRf", q, 1), Op.mult)
+    mm(w("UW", 0, 128), v("BLK"), v("IJD"), True, True)
+    ts(v("M7"), c128, 7, Op.bitwise_and)
+    ts(v("cX"), SP, 8.0, Op.is_ge, 100.0, Op.mult)
+    ts(w("SPm", 1, 1), SP, -8.0, Op.add)
+    tt(w("SPm", 0, 1), SP, v("cX"), Op.add)
+    ts(v("IDf"), c128, PI, Op.is_equal)
+    ts(v("ID"), c128, PI, Op.is_equal)
+    ts(v("I2"), c128, PI, Op.is_equal, 2.0, Op.mult)
+    vc(w("IJ", 0, 128), w("UW", 0, 128))
+    ts(w("I2h", 0, 128), w("MS", 0, 128), 8.0, Op.is_lt)
+    ts(w("I2h", 128, 128), w("MS", 0, 128), 8.0, Op.is_ge)
+    for p in range(2):
+        ts(w("TMP", 128 * p, 128), v("M7"), w("SPm", p, 1), Op.is_equal, 2.0, Op.mult)
+        ts(w("TMP", 256 + 128 * p, 128), w("MS", 0, 128), w("SPm", p, 1), Op.is_equal)
+        tt(w("TMP", 128 * p, 128), w("TMP", 128 * p, 128), v("BLK"), Op.mult)
+        tt(w("M2S", 128 * p, 128), w("TMP", 256 + 128 * p, 128), v("BLK"), Op.mult)
+        for h in range(2): tt(w("DUP", 256 * p + 128 * h, 128), w("TMP", 128 * p, 128), w("I2h", 128 * h, 128), Op.mult)
+    for h in range(2): tt(w("I2h", 128 * h, 128), w("I2h", 128 * h, 128), v("I2"), Op.mult)
+    for h, name in ((0, "EI"), (1, "EJ")):
+        ts(w("TMP", 128 * h, 128), w("MS", 0, 128), 8.0 + h, Op.is_equal)
+        tt(v(name), w("TMP", 128 * h, 128), v("ID"), Op.mult)
+    ts(v("M8"), w("CI", 0, 64), 3, Op.logical_shift_right)
+    ts(v("M1"), v("CI", 0, 128, 1, 8), 1, Op.bitwise_and)
+    ts(v("MH"), v("CI", 0, 128, 1, 64), 1, Op.logical_shift_right)
+    p64, p8 = v("PIf", 0, 1, 1, 64), v("PIf", 0, 1, 1, 8)
+    ts(v("EXp"), v("MH"), p64, Op.is_equal, 64.0, Op.mult)
+    ts(v("EXf"), v("MH"), p64, Op.is_equal, BAD, Op.mult)
+    ts(v("INDF"), v("M8"), GP_, Op.is_equal, BAD, Op.mult)
+    ts(v("INDP"), v("M8"), GP_, Op.is_equal, 64.0, Op.mult)
+    ts(v("IND1"), v("M8"), GP_, Op.is_equal)
+    ts(v("LIDX"), v("M1", 0, 128, 1, 2), v("PIf", 0, 1, 1, 2), Op.is_equal)
+    ts(w("MM", 0, 64), v("ND"), 128.0, Op.add)
+
+    def late_constants():
+        ts(v("C63"), v("CI"), 63, Op.bitwise_and)
+        ts(v("RS16"), v("MS"), 0.0, Op.is_gt)
+        ts(v("RS2"), v("M1"), 0.0, Op.is_equal, BAD, Op.mult)
+        ts(v("E8"), v("MG", 0, 128, 1, 8), p8, Op.is_equal)
+        ts(v("E8o"), v("MG", 0, 128, 1, 8), p8, Op.is_equal, OUT, Op.mult)
+        ts(v("ownA"), SP, 8.0, Op.mult)
+        ts(v("ownT"), SP, 8.0, Op.is_ge, 2 * BAD, Op.mult)
+        ts(v("RS64"), v("C63"), 0.0, Op.is_equal, BIG, Op.mult)
+        tt(v("ownB"), SP, v("ownT"), Op.add)
+        ts(v("ownB"), v("ownB"), BAD, Op.min)
+        ts(v("cW"), SP, 8.0, Op.is_le)
+        ts(v("cJ"), SP, 9.0, Op.is_equal)
+        ts(v("TRI"), v("TI"), SP, Op.is_ge, 32768.0, Op.mult)
+        ts(v("DUM"), v("DI"), SP, Op.add)
+        ts(v("SELW"), v("BLK"), v("cW"), Op.mult)
+        ts(v("SELJ"), v("BLK"), v("cJ"), Op.mult)
+        for s in range(8, 16): ts(w("SEL", 128 * s, 128), v("BLK"), w("SPQ", s, 1), Op.mult)
+
+    one1 = v("ONE", 0, 128, 1, 1)
+    BANKS = ("XB0", "XB1", "KT")
+    ORDER = [0, 1, 2, 3, 8, 9, 4, 5, 6, 7]
+    for t in range(RO):
+        par, last = t % 2, t == RO - 1
+        jw, iw = w("IJ", 128 * t, 64), w("IJ", 128 * t + 64, 64)
+        need = w("MM", 64 * t, 64)
+        if t:
+            landed("l", t, "LL", 8); landed("i", t, "IJ", 128); landed("n", t, "MM", 64)
+
+        for h in range(2): mm(w("XB%d" % h, 0, 256), one1, v("XPRE"), True, False)
+        vc(v("Xf"), ix("CM", 2048, w("LL", 8 * t, 4)))
+        ts(v("Yp"), ix("RM", 1536, w("LL", 8 * t + 4, 4)), 2.0, Op.mult, 593.0, Op.add)
+        for b in range(8): mm(w("XB%d" % (b // 4), 64 * (b % 4), 64), w("SEL", 128 * (8 * par + b), 128), v("Xf"), False, b % 4 == 3)
+
+        def prod(b): tt(w("Pc", 64 * b, 64), w("XB%d" % (b // 4), 64 * (b % 4), 64), v("Yp"), Op.mult)
+        def shift(lo, hi): ts(v("Pi", lo, hi), v("Pc", lo, hi), 5, Op.logical_shift_right, W - 1, Op.bitwise_and)
+        def conv(lo, hi): vc(v("OF", lo, hi), v("Pi", lo, hi))
+
+        for b in range(4): prod(b)
+        shift(0, 128)
+        for b in range(4, 8): prod(b)
+        conv(0, 128)
+        shift(128, 512)
+        conv(128, 512)
+        if t == 0: late_constants()
+        mm(w("JI", 0, 160), v("ONE"), v("JPRE"), True, False)
+        mm(w("KT", 0, 32), one1, v("XPRE", 0, 32), True, False)
+        mm(key(T.KEY[:]), v("LIDX"), v("IDXR"), True, False)
+        for h in range(2): mm(w("KT", 0, 32), w("DUP", 256 * par + 128 * h, 128), v("Xf", h, 64, 2), False, h == 1)
+        mm(w("MB", 320, 64), w("M2S", 128 * par, 128), v("Xf"), True, False)
+        mm(w("JI", 0, 64), v("I2"), iw, False, False)
+        mm(w("JI", 64, 64), v("I2"), jw, False, False)
+        for h in range(2): mm(w("JI", 128, 32), w("I2h", 128 * h, 128), v("IJ", 128 * t + h, 128 * t + 64, 2), False, h == 1)
+        mm(w("MB", 320, 64), v("EI"), iw, False, False)
+        mm(w("MB", 320, 64), v("EJ"), jw, False, True)
+        for a in range(16): act(v("NR", a, 1024, 16), need, bias=-128.0)
+        act(w("FA", W, P), need, scale=2.0, bias=-255.0)
+
+        def pos(lo, hi):
+            out, off = (v("GP2"), v("OF", 576, 608)) if lo == 9 else (v("GP", 1024 * lo, 1024 * hi), v("OF", 64 * lo, 64 * hi))
+            act(out, ix("PP" if t else "FA", W, off), scale=1.0 if t else 2.0)
+        def fails(b):
+            if b == 9: tt(v("GF2"), ix("FA", W, v("OF", 576, 608)), v("NR", 0, 1024, 2), Op.is_lt)
+            else: tt(w("GF", 1024 * b, 1024), ix("FA", W, w("OF", 64 * b, 64)), v("NR"), Op.is_lt)
+        def keys(which):
+            for b in which:
+                for n, bank in (("P", "UW"), ("F", "TAB")):
+                    for c in range(8):
+                        if b < 8:
+                            mm(key(T.KEY[:, :, 8 * b + c]), v("G" + n, 1024 * b + c, 1024 * b + 1024, 8), v("IND" + n, 0, 64, 8), False, (n, b, c) == ("F", 7, 7))
+                        elif b == 8:
+                            mm(key(T.KEY[:, :, c:64:8]), v("G" + n, 8192 + c, 9216, 8), v("IND" + n), False, False)
+                        else:
+                            mm(v(bank, 256 + c, 320, 8, 64), v("G" + n + "2", c, 512, 8), v("IND1", 0, 64, 8), True, True)
+
+        pos(0, 1); pos(1, 2)
+        act(v("Y2"), w("JI", 128, 32))
+        fails(0); fails(1)
+        tt(w("Pc", 512, 64), w("JI", 0, 64), v("Yp"), Op.mult)
+        tt(w("Pc", 576, 32), w("KT", 0, 32), v("Y2"), Op.mult)
+        shift(512, 608)
+        conv(512, 608)
+        pos(2, 4); pos(8, 9); pos(9, 10); pos(4, 6)
+        for b in ORDER[2:7]: fails(b)
+        keys(ORDER[0:7])
+        act(v("C2f"), v("TAB", 256, 320, 1, 64))
+        vc(v("C2p"), v("UW", 256, 320, 1, 64))
+        pos(6, 7); pos(7, 8)
+        for b in ORDER[7:]: fails(b)
+        for c in range(8):
+            mm(key(T.KEY[:, :, c:64:8]), v("EXp"), v("C2p"), False, False)
+            mm(key(T.KEY[:, :, c:64:8]), v("EXf"), v("C2f"), False, False)
+        keys(ORDER[7:])
+        act(w("YM", 0, 64), v("Yp"), bias=-296.5, scale=0.5)
+        act(w("YM", 64, 64), w("MB", 320, 64))
+        if t == 0: act(v("PP", 0, W), v("FA", 0, W), scale=2.0)
+
+        for k in range(8): do("V", g.vector.tensor_reduce, w("S1", k, 1), [key(None)], (T.KEY[:, k, :], AxisListType.X, Op.min))
+        kt = v("KT", 128, 256, 1, 8)
+        mm(kt, v("S1"), v("IDf"), True, True)
+        km = v("KM", 128 * t + 1, 128 * t + 128, 2)
+        scan(w("KM", 128 * t, 128), v("RS2"), kt, Op.max, Op.min)
+        ts(w("T32", 0, 64), km, 0x7FF00078, Op.bitwise_and)
+        ts(w("T32", 64, 64), km, 0x7FF00007, Op.bitwise_and)
+        vc(v("TBf"), v("T32"))
+        ts(v("B01"), km, BAD, Op.is_ge)
+        mm(w("TAB", 0, 128), v("E8"), v("TBf"), True, True)
+        mm(w("MB", 0, 192), one1, v("MPRE"), True, False)
+        for k in range(3): mm(w("MB", 64 * k, 64), v("E8o"), v("B01"), False, k == 2)
+        ts(w("KT", 256, 64), w("TAB", 0, 64), v("ownA"), Op.is_equal)
+        ts(w("KT", 320, 64), w("TAB", 64, 64), v("ownB"), Op.is_equal)
+        tt(v("UAW"), w("KT", 256, 128), v("YM"), Op.mult)
+        for bank, o in (("UW", 0), ("MB", 192)):
+            mm(w(bank, o, 64), v("BLK"), w("UAW", 0, 64), True, False)
+            mm(w(bank, o, 64), v("SELJ"), w("UAW", 64, 64), False, True)
+            mm(w(bank, o + 64, 64), v("SELW"), w("UAW", 64, 64), True, True)
+        for bank in BANKS: mm(w(bank, 0, 256), v("ID"), v("TRI"), True, False)
+        tt(v("LD"), w("UW", 0, 128), w("DIAG", 0, 128), Op.mult)
+        scan(v("LSc"), w("RS16", 0, 128), v("LD"), Op.mult, Op.add)
+        vc(w("LS", 8 * t, 8), v("LSc", 15, 128, 16))
+        send("l", t, w("LL", 8 * t + 8, 8), w("LS", 8 * t, 8))
+
+        act(w("UWs", 0, 64), w("MB", 192, 64), scale=2.0, bias=593.0)
+        act(w("UWs", 64, 64), w("MB", 256, 64), scale=2.0, bias=17.0)
+
+        def targets(lo, hi):
+            ts(v("FI", lo, hi), v("PF", lo, hi), 5, Op.logical_shift_right, W - 1, Op.bitwise_and)
+            tt(v("TAB", 192 + lo, 192 + hi), v("FI", lo, hi), v("MB", lo, hi), Op.add)
+            tt(v("VD", lo, hi), v("TAB", 192 + lo, 192 + hi), v("DIAG", lo, hi), Op.mult)
+            scan(v("SL", lo, hi), v("RS16", lo, hi), v("VD", lo, hi), Op.mult, Op.add)
+
+        def compare(ty):
+            for q in range(4): mm(w(BANKS[ty], 64 * q, 64), v("BLK"), w("VD", 64 * ty, 64), False, q == 3)
+            for q in range(4):
+                c = 4 * ty + q
+                act(w("AB", 64 * c, 64), w(BANKS[ty], 64 * q, 64), Act.Abs, scale=-1.0, bias=w("SL", 16 * c + 15, 1))
+
+        def needs():
+            tt(v("TN"), v("SL", 15, 64, 16), w("DUM", 0, 4), Op.min)
+            ts(v("TNu"), v("TN"), 2048.0, Op.add)
+            ts(w("NS", 64 * t, 64), ix("FA", W + P, v("TNu")), 0.5, Op.mult, 127.75, Op.add)
+            send("n", t, w("MM", 64 * t + 64, 64), w("NS", 64 * t, 64))
+
+        tt(w("PF", 0, 64), w("UWs", 0, 64), w("UWs", 64, 64), Op.mult)
+        targets(0, 64)
+        compare(0)
+        tt(w("PF", 64, 128), v("UWs"), w("JI", 0, 128), Op.mult)
+        if not last: needs()
+
+        targets(64, 192)
+        compare(1)
+        compare(2)
+        if not last:
+            vc(w("IS", 128 * t, 128), w("UW", 0, 128))
+            send("i", t, w("IJ", 128 * t + 128, 128), w("IS", 128 * t, 128))
+            act(w("NA", 1024 * t, 1024), w("FA", 1024 * t, 1024), scale=-1.0)
+        scan(v("MN"), v("RS64"), v("AB"), Op.max, Op.min)
+        ts(v("DU"), v("MN", 63, 768, 64), 0.0, Op.is_equal, OUT, Op.mult)
+        tt(v("DV"), v("DU"), v("SL", 15, 192, 16), Op.add)
+        tt(v("DW"), v("DV"), v("DUM"), Op.min)
+        ts(v("TS"), v("DW"), 2048.0, Op.add)
+        for ty in range(3): vc(ix("PP", W + P, w("TS", 4 * ty, 4)), v("ZER"))
+        y1, y2 = ext(T.yf[:, 0:W - ROT], "yf1"), ext(T.yf[:, W - ROT:W], "yf2")
+        if t == RO - 2:
+            dma("P", "gd", 32, y1, v("NA", ROT, W))
+            dma("P", "gd", 32, y2, v("NA", 0, ROT))
+        if last:
+            dma("P", "gd2", 32, y1, v("PP", ROT, W), accum_op=Op.add, max_dma_last_dim=4096)
+            dma("P", "gd2", 32, y2, v("PP", 0, ROT), accum_op=Op.add, max_dma_last_dim=4096)
+            needs()
+
+    ts(v("YI"), v("KM", 1, 640, 2), 7, Op.logical_shift_right)
+    ts(v("YT"), v("YI"), 8192.0, Op.is_ge, -8193.0, Op.mult)
+    tt(v("YC"), v("YI"), v("YT"), Op.add)
+    dma("D", "out", 48, ext(T.yc[:], "yc"), v("YC"))
+    landed("l", RO, "LL", 8); landed("n", RO, "MM", 64)
+    vc(w("YPo", 0, 4), w("LL", 44, 4))
+    vc(w("YPo", 4, 4), w("LL", 40, 4))
+    ts(v("YZo"), w("MM", 320, 64), -128.0, Op.add)
+    dma("D", "out", 48, ext(T.yp[:], "yp"), v("YPo"))
+    dma("D", "out", 48, ext(T.yz[:], "yz"), v("YZo"))
+    wait("P", "ls", sent[0])
+    wait("P", "gd2", 32)
+    wait("D", "out", 48)
+    for q in "VSTP": wait("D", q, cnt[q])

@@ -15,13 +15,14 @@ def _bufs(dtype, text, where="sbuf"):
 
 
 _bufs("bfloat16", "GF2 512, GP2 512, C2f 64 64, EXf 128 64, FA 4160, PP 4160, NA 4096, ND 64, MM 384, NS 320, NR 1024, GF 9216, GP 9216, AB 768, MN 768, ZER 64, YZo 64")
-_bufs("bfloat16", "TBf 128 8, B01 64 8, E8 128 8, E8o 128 8, LIDX 128 2, IDXR 512 2, INDF 64, INDP 64, IND1 64, DIAG 192, RS16 192, RS64 768, ONE 128 2, XPRE 256 1, JPRE 160 2, MPRE 192 1")
-_bufs("int32", "RM 1536, CM 2048, PR 8, PI 1, CI 768, TI 256, DI 12, GPi 1, SPi 1, MG 128, MS 192, M7 128, M1 128 8, MH 128 64, M8 64, C63 768, Pc 608, Pi 608, KM 640 8, T32 128 8, PF 192, FI 192, YI 320 8")
+_bufs("bfloat16", "TBf 32, E8 512, LIDX 128 2, IDXR 512 2, INDF 64, INDP 64, IND1 64, DIAG 192, RS16 192, RS64 768, ONE 128 2, XPRE 256 1, JPRE 160 2, MPRE 192 1")
+_bufs("int32", "RM 1536, CM 2048, PR 8, PI 1, QI 4, CI 192, TI 256, DI 12, GPi 1, SPi 1, MG 128, MS 192, M7 128, M1 128, MH 128 64, M8 64, Pc 608, Pi 608, KM 160, T32 32, PF 192, FI 192, YI 80")
 _bufs("uint16", "LL 48, LS 40, OF 608, TNu 4, TS 12")
-_bufs("float16", "C2p 64 64, EXp 128 64, IJ 768, IS 640, IJD 128, BLK 128, SEL 2048, DUP 512, M2S 256, TMP 512, ID 128, I2 128, I2h 256, EI 128, EJ 128, SELW 128, SELJ 128, TRI 256, Xf 64, UAW 128, VD 192")
-_bufs("float32", "PRf 8, GPf 1, SPf 1, PIf 1, SPQ 16, SPm 2, IDf 128, cX 1, cW 1, cJ 1, ownA 1, ownB 1, ownT 1, RS2 128 8, DUM 12, Yp 64, YM 128, Y2 32, S1 8, LD 128, LSc 128, UWs 128, SL 192, TN 4, DU 12, DV 12, DW 12, YT 320 8, YC 320 8, YPo 8")
+_bufs("float16", "C2p 64 64, EXp 128 64, IJ 768, IS 640, IJD 128, BLK 128, BLKo 128, SEL 2048, DUP 512, M2S 256, TMP 512, ID 128, I2 128, I2h 256, EI 128, EJ 128, SELW 128, SELJ 128, TRI 256, Xf 64, UAW 128, B01 64, VD 192")
+_bufs("float32", "PRf 8, GPf 1, SPf 1, PIf 1, QP 4, SPQ 16, SPm 2, SY 32, cX 1, cW 1, cJ 1, ownA 1, ownB 1, ownT 1, RS2 32, DUM 12, Yp 64, YM 128, Y2 32, S1 32, ST 32, LD 128, LSc 128, UWs 128, SL 192, TN 4, DU 12, DV 12, DW 12, YT 80, YC 80, YPo 8")
 _bufs("float32", "XB0 512, XB1 512, JI 512, MB 512, KT 512, TAB 512, UW 512, KEY 512", "psum")
 SCRATCH["KEY"] = ("psum", [128, 8, 64], "float32")
+SCRATCH["YO"] = ("sbuf", [8, 4, 80], "float32")
 SEMAPHORES = ["sV", "sS", "sT", "sP", "ls", "out", "gd", "gd2"] + ["ld%d" % k for k in range(7)] + ["%s%d" % (m, t) for m in "lin" for t in range(1, RO + 1)]
 
 
@@ -112,35 +113,33 @@ def rank_program(g, core, T, topo):
     dma("D", "ld6", 16, v("FA", 0, ROT), ext(T.fig[:, W - ROT:W]))
 
     iota("PI", [[0, 1]], 0, 1)
-    iota("CI", [[1, 768]], 0, 0)
+    iota("CI", [[1, 192]], 0, 0)
+    iota("QI", [[-32, 4]], 0, 1)
+    fill(v("RS64"), BIG)
     iota("IDXR", [[0, 8], [1, 8], [8, 8]], 0, 64, allow_small_or_imprecise_dtypes=True)
     iota("TI", [[-16, 4], [1, 64]], 0, 0)
     iota("DI", [[0, 3], [16, 4]], W - 2048, 0)
-    for name, c in (("ONE", 1.0), ("XPRE", 17.0), ("JPRE", 1.0), ("MPRE", -2048.0), ("ZER", 0.0)): fill(v(name), c)
+    do("P", g.affine_select, v("RS64"), [v("RS64")], (T.RS64[:], [[0, 12], [1, 64]], Op.is_equal, 0.0, 0, 0))
+    for name, c in (("ONE", 1.0), ("XPRE", 17.0), ("JPRE", 1.0), ("MPRE", -2048.0), ("ZER", 0.0), ("S1", 0.0)): fill(v(name), c)
     fill(v("JPRE", 0, 64, 1, 1), 16.0)
     fill(v("JPRE", 64, 160, 1, 1), 592.0)
     c128, SP, GP_, PI = v("CI", 0, 128), v("SPf"), v("GPf"), v("PIf")
     ts(v("SPi"), v("PI"), 15, Op.bitwise_and)
     ts(v("GPi"), v("PI"), 4, Op.logical_shift_right)
     ts(v("MG"), c128, 4, Op.logical_shift_right)
-    ts(v("MS"), v("CI", 0, 192), 15, Op.bitwise_and)
-    vc(SP, v("SPi")); vc(GP_, v("GPi")); vc(PI, v("PI"))
+    ts(v("MS"), v("CI"), 15, Op.bitwise_and)
+    vc(SP, v("SPi")); vc(GP_, v("GPi")); vc(PI, v("PI")); vc(v("QP"), v("QI"))
     ts(v("BLK"), v("MG"), GP_, Op.is_equal)
     ts(v("SPQ"), v("CI", 0, 16), SP, Op.is_equal, 2.0, Op.mult)
-    for s in range(8): ts(w("SEL", 128 * s, 128), v("BLK"), w("SPQ", s, 1), Op.mult)
     ts(v("DIAG"), v("MS"), SP, Op.is_equal)
-    vc(w("LL", 0, 8), v("PR"))
-    vc(v("PRf"), v("PR"))
-    for q in range(8): ts(w("IJD", 16 * q, 16), w("DIAG", 0, 16), w("PRf", q, 1), Op.mult)
-    mm(w("UW", 0, 128), v("BLK"), v("IJD"), True, True)
     ts(v("M7"), c128, 7, Op.bitwise_and)
+    ts(v("M1"), c128, 1, Op.bitwise_and)
+    for s in range(8): ts(w("SEL", 128 * s, 128), v("BLK"), w("SPQ", s, 1), Op.mult)
     ts(v("cX"), SP, 8.0, Op.is_ge, 100.0, Op.mult)
     ts(w("SPm", 1, 1), SP, -8.0, Op.add)
     tt(w("SPm", 0, 1), SP, v("cX"), Op.add)
-    ts(v("IDf"), c128, PI, Op.is_equal)
     ts(v("ID"), c128, PI, Op.is_equal)
     ts(v("I2"), c128, PI, Op.is_equal, 2.0, Op.mult)
-    vc(w("IJ", 0, 128), w("UW", 0, 128))
     ts(w("I2h", 0, 128), w("MS", 0, 128), 8.0, Op.is_lt)
     ts(w("I2h", 128, 128), w("MS", 0, 128), 8.0, Op.is_ge)
     for p in range(2):
@@ -154,39 +153,41 @@ def rank_program(g, core, T, topo):
         ts(w("TMP", 128 * h, 128), w("MS", 0, 128), 8.0 + h, Op.is_equal)
         tt(v(name), w("TMP", 128 * h, 128), v("ID"), Op.mult)
     ts(v("M8"), w("CI", 0, 64), 3, Op.logical_shift_right)
-    ts(v("M1"), v("CI", 0, 128, 1, 8), 1, Op.bitwise_and)
     ts(v("MH"), v("CI", 0, 128, 1, 64), 1, Op.logical_shift_right)
-    p64, p8 = v("PIf", 0, 1, 1, 64), v("PIf", 0, 1, 1, 8)
+    p64 = v("PIf", 0, 1, 1, 64)
     ts(v("EXp"), v("MH"), p64, Op.is_equal, 64.0, Op.mult)
     ts(v("EXf"), v("MH"), p64, Op.is_equal, BAD, Op.mult)
     ts(v("INDF"), v("M8"), GP_, Op.is_equal, BAD, Op.mult)
     ts(v("INDP"), v("M8"), GP_, Op.is_equal, 64.0, Op.mult)
     ts(v("IND1"), v("M8"), GP_, Op.is_equal)
     ts(v("LIDX"), v("M1", 0, 128, 1, 2), v("PIf", 0, 1, 1, 2), Op.is_equal)
+    vc(w("LL", 0, 8), v("PR"))
+    vc(v("PRf"), v("PR"))
+    for q in range(8): ts(w("IJD", 16 * q, 16), w("DIAG", 0, 16), w("PRf", q, 1), Op.mult)
+    mm(w("UW", 0, 128), v("BLK"), v("IJD"), True, True)
     ts(w("MM", 0, 64), v("ND"), 128.0, Op.add)
+    for q in range(4): ts(w("E8", 128 * q, 128), v("MG"), w("QP", q, 1), Op.is_equal)
+    vc(w("IJ", 0, 128), w("UW", 0, 128))
+    ts(v("RS16"), v("MS"), 0.0, Op.is_gt)
+    ts(v("RS2"), w("M1", 0, 32), 0.0, Op.is_equal, BAD, Op.mult)
+    ts(v("ownA"), SP, 8.0, Op.mult)
+    ts(v("ownT"), SP, 8.0, Op.is_ge, 2 * BAD, Op.mult)
+    ts(v("cW"), SP, 8.0, Op.is_le)
+    tt(v("ownB"), SP, v("ownT"), Op.add)
+    ts(v("cJ"), SP, 9.0, Op.is_equal)
+    ts(v("ownB"), v("ownB"), BAD, Op.min)
+    ts(v("SELW"), v("BLK"), v("cW"), Op.mult)
+    ts(v("SELJ"), v("BLK"), v("cJ"), Op.mult)
+    ts(v("BLKo"), v("BLK"), OUT / 16, Op.mult)
 
     def late_constants():
-        ts(v("C63"), v("CI"), 63, Op.bitwise_and)
-        ts(v("RS16"), v("MS"), 0.0, Op.is_gt)
-        ts(v("RS2"), v("M1"), 0.0, Op.is_equal, BAD, Op.mult)
-        ts(v("E8"), v("MG", 0, 128, 1, 8), p8, Op.is_equal)
-        ts(v("E8o"), v("MG", 0, 128, 1, 8), p8, Op.is_equal, OUT, Op.mult)
-        ts(v("ownA"), SP, 8.0, Op.mult)
-        ts(v("ownT"), SP, 8.0, Op.is_ge, 2 * BAD, Op.mult)
-        ts(v("RS64"), v("C63"), 0.0, Op.is_equal, BIG, Op.mult)
-        tt(v("ownB"), SP, v("ownT"), Op.add)
-        ts(v("ownB"), v("ownB"), BAD, Op.min)
-        ts(v("cW"), SP, 8.0, Op.is_le)
-        ts(v("cJ"), SP, 9.0, Op.is_equal)
         ts(v("TRI"), v("TI"), SP, Op.is_ge, 32768.0, Op.mult)
         ts(v("DUM"), v("DI"), SP, Op.add)
-        ts(v("SELW"), v("BLK"), v("cW"), Op.mult)
-        ts(v("SELJ"), v("BLK"), v("cJ"), Op.mult)
         for s in range(8, 16): ts(w("SEL", 128 * s, 128), v("BLK"), w("SPQ", s, 1), Op.mult)
+        for q in range(4): ts(w("SY", 8 * q, 8), v("CI", 0, 8), w("QP", q, 1), Op.is_equal)
 
     one1 = v("ONE", 0, 128, 1, 1)
     BANKS = ("XB0", "XB1", "KT")
-    ORDER = [0, 1, 2, 3, 8, 9, 4, 5, 6, 7]
     for t in range(RO):
         par, last = t % 2, t == RO - 1
         jw, iw = w("IJ", 128 * t, 64), w("IJ", 128 * t + 64, 64)
@@ -209,7 +210,6 @@ def rank_program(g, core, T, topo):
         conv(0, 128)
         shift(128, 512)
         conv(128, 512)
-        if t == 0: late_constants()
         mm(w("JI", 0, 160), v("ONE"), v("JPRE"), True, False)
         mm(w("KT", 0, 32), one1, v("XPRE", 0, 32), True, False)
         mm(key(T.KEY[:]), v("LIDX"), v("IDXR"), True, False)
@@ -247,40 +247,42 @@ def rank_program(g, core, T, topo):
         tt(w("Pc", 576, 32), w("KT", 0, 32), v("Y2"), Op.mult)
         shift(512, 608)
         conv(512, 608)
-        pos(2, 4); pos(8, 9); pos(9, 10); pos(4, 6)
-        for b in ORDER[2:7]: fails(b)
-        keys(ORDER[0:7])
+        pos(2, 3); pos(8, 9); pos(9, 10); pos(3, 5)
+        for b in (2, 8, 9, 3): fails(b)
+        keys((0, 1, 2, 8, 9, 3))
         act(v("C2f"), v("TAB", 256, 320, 1, 64))
         vc(v("C2p"), v("UW", 256, 320, 1, 64))
-        pos(6, 7); pos(7, 8)
-        for b in ORDER[7:]: fails(b)
+        pos(5, 7); pos(7, 8)
+        for b in (4, 5, 6, 7): fails(b)
         for c in range(8):
             mm(key(T.KEY[:, :, c:64:8]), v("EXp"), v("C2p"), False, False)
             mm(key(T.KEY[:, :, c:64:8]), v("EXf"), v("C2f"), False, False)
-        keys(ORDER[7:])
+        keys((4, 5, 6, 7))
         act(w("YM", 0, 64), v("Yp"), bias=-296.5, scale=0.5)
         act(w("YM", 64, 64), w("MB", 320, 64))
+        mm(w("MB", 0, 192), one1, v("MPRE"), True, False)
         if t == 0: act(v("PP", 0, W), v("FA", 0, W), scale=2.0)
 
         for k in range(8): do("V", g.vector.tensor_reduce, w("S1", k, 1), [key(None)], (T.KEY[:, k, :], AxisListType.X, Op.min))
-        kt = v("KT", 128, 256, 1, 8)
-        mm(kt, v("S1"), v("IDf"), True, True)
-        km = v("KM", 128 * t + 1, 128 * t + 128, 2)
-        scan(w("KM", 128 * t, 128), v("RS2"), kt, Op.max, Op.min)
-        ts(w("T32", 0, 64), km, 0x7FF00078, Op.bitwise_and)
-        ts(w("T32", 64, 64), km, 0x7FF00007, Op.bitwise_and)
+        do("V", g.vector.transpose, v("ST"), [v("S1")], (T.S1[:],))
+        scan(w("KM", 32 * t, 32), v("RS2"), v("ST"), Op.max, Op.min)
+        km = v("KM", 32 * t + 1, 32 * t + 32, 2)
+        ts(v("T32", 0, 32, 2), km, 0x7FF00078, Op.bitwise_and)
+        ts(v("T32", 1, 32, 2), km, 0x7FF00007, Op.bitwise_and)
         vc(v("TBf"), v("T32"))
-        ts(v("B01"), km, BAD, Op.is_ge)
-        mm(w("TAB", 0, 128), v("E8"), v("TBf"), True, True)
-        mm(w("MB", 0, 192), one1, v("MPRE"), True, False)
-        for k in range(3): mm(w("MB", 64 * k, 64), v("E8o"), v("B01"), False, k == 2)
-        ts(w("KT", 256, 64), w("TAB", 0, 64), v("ownA"), Op.is_equal)
-        ts(w("KT", 320, 64), w("TAB", 64, 64), v("ownB"), Op.is_equal)
+        for q in range(4): mm(w("TAB", 32 * q, 32), w("E8", 128 * q, 128), v("TBf"), True, True)
+        ts(w("KT", 256, 64), v("TAB", 0, 128, 2), v("ownA"), Op.is_equal)
+        ts(w("KT", 320, 64), v("TAB", 1, 128, 2), v("ownB"), Op.is_equal)
+        ts(v("B01"), v("TAB", 1, 128, 2), BAD, Op.is_ge)
         tt(v("UAW"), w("KT", 256, 128), v("YM"), Op.mult)
-        for bank, o in (("UW", 0), ("MB", 192)):
+        def names(bank, o):
             mm(w(bank, o, 64), v("BLK"), w("UAW", 0, 64), True, False)
             mm(w(bank, o, 64), v("SELJ"), w("UAW", 64, 64), False, True)
             mm(w(bank, o + 64, 64), v("SELW"), w("UAW", 64, 64), True, True)
+        names("UW", 0)
+        for k in range(3): mm(w("MB", 64 * k, 64), v("BLKo"), v("B01"), False, k == 2)
+        names("MB", 192)
+        if t == 0: late_constants()
         for bank in BANKS: mm(w(bank, 0, 256), v("ID"), v("TRI"), True, False)
         tt(v("LD"), w("UW", 0, 128), w("DIAG", 0, 128), Op.mult)
         scan(v("LSc"), w("RS16", 0, 128), v("LD"), Op.mult, Op.add)
@@ -289,44 +291,46 @@ def rank_program(g, core, T, topo):
 
         act(w("UWs", 0, 64), w("MB", 192, 64), scale=2.0, bias=593.0)
         act(w("UWs", 64, 64), w("MB", 256, 64), scale=2.0, bias=17.0)
+        def f_col(k): ts(w("FI", 64 * k, 64), w("PF", 64 * k, 64), 5, Op.logical_shift_right, W - 1, Op.bitwise_and)
+        def f_out(k): tt(w("TAB", 192 + 64 * k, 64), w("FI", 64 * k, 64), w("MB", 64 * k, 64), Op.add)
+        def f_own(k): tt(w("VD", 64 * k, 64), w("TAB", 192 + 64 * k, 64), w("DIAG", 0, 64), Op.mult)
+        def f_list(k): scan(w("SL", 64 * k, 64), w("RS16", 0, 64), w("VD", 64 * k, 64), Op.mult, Op.add)
 
-        def targets(lo, hi):
-            ts(v("FI", lo, hi), v("PF", lo, hi), 5, Op.logical_shift_right, W - 1, Op.bitwise_and)
-            tt(v("TAB", 192 + lo, 192 + hi), v("FI", lo, hi), v("MB", lo, hi), Op.add)
-            tt(v("VD", lo, hi), v("TAB", 192 + lo, 192 + hi), v("DIAG", lo, hi), Op.mult)
-            scan(v("SL", lo, hi), v("RS16", lo, hi), v("VD", lo, hi), Op.mult, Op.add)
-
-        def compare(ty):
-            for q in range(4): mm(w(BANKS[ty], 64 * q, 64), v("BLK"), w("VD", 64 * ty, 64), False, q == 3)
+        def compare(k):
+            for q in range(4): mm(w(BANKS[k], 64 * q, 64), v("BLK"), w("VD", 64 * k, 64), False, q == 3)
             for q in range(4):
-                c = 4 * ty + q
-                act(w("AB", 64 * c, 64), w(BANKS[ty], 64 * q, 64), Act.Abs, scale=-1.0, bias=w("SL", 16 * c + 15, 1))
+                c = 4 * k + q
+                act(w("AB", 64 * c, 64), w(BANKS[k], 64 * q, 64), Act.Abs, scale=-1.0, bias=w("SL", 16 * c + 15, 1))
 
-        def needs():
-            tt(v("TN"), v("SL", 15, 64, 16), w("DUM", 0, 4), Op.min)
-            ts(v("TNu"), v("TN"), 2048.0, Op.add)
+        def need1(): tt(v("TN"), v("SL", 15, 64, 16), w("DUM", 0, 4), Op.min)
+        def need2(): ts(v("TNu"), v("TN"), 2048.0, Op.add)
+        def need3():
             ts(w("NS", 64 * t, 64), ix("FA", W + P, v("TNu")), 0.5, Op.mult, 127.75, Op.add)
             send("n", t, w("MM", 64 * t + 64, 64), w("NS", 64 * t, 64))
 
         tt(w("PF", 0, 64), w("UWs", 0, 64), w("UWs", 64, 64), Op.mult)
-        targets(0, 64)
-        compare(0)
         tt(w("PF", 64, 128), v("UWs"), w("JI", 0, 128), Op.mult)
-        if not last: needs()
-
-        targets(64, 192)
+        f_col(0); f_col(1); f_out(0); f_col(2); f_own(0); f_out(1); f_list(0); f_own(1)
+        compare(0)
+        if not last: need1()
+        f_list(1)
         compare(1)
+        if not last: need2()
+        f_out(2)
+        if not last: need3()
+        f_own(2); f_list(2)
         compare(2)
+
         if not last:
             vc(w("IS", 128 * t, 128), w("UW", 0, 128))
             send("i", t, w("IJ", 128 * t + 128, 128), w("IS", 128 * t, 128))
             act(w("NA", 1024 * t, 1024), w("FA", 1024 * t, 1024), scale=-1.0)
-        scan(v("MN"), v("RS64"), v("AB"), Op.max, Op.min)
+        for lo, n in ((0, 512), (512, 256)): scan(w("MN", lo, n), w("RS64", lo, n), w("AB", lo, n), Op.max, Op.min)
         ts(v("DU"), v("MN", 63, 768, 64), 0.0, Op.is_equal, OUT, Op.mult)
         tt(v("DV"), v("DU"), v("SL", 15, 192, 16), Op.add)
         tt(v("DW"), v("DV"), v("DUM"), Op.min)
         ts(v("TS"), v("DW"), 2048.0, Op.add)
-        for ty in range(3): vc(ix("PP", W + P, w("TS", 4 * ty, 4)), v("ZER"))
+        for k in range(3): vc(ix("PP", W + P, w("TS", 4 * k, 4)), v("ZER"))
         y1, y2 = ext(T.yf[:, 0:W - ROT], "yf1"), ext(T.yf[:, W - ROT:W], "yf2")
         if t == RO - 2:
             dma("P", "gd", 32, y1, v("NA", ROT, W))
@@ -334,19 +338,22 @@ def rank_program(g, core, T, topo):
         if last:
             dma("P", "gd2", 32, y1, v("PP", ROT, W), accum_op=Op.add, max_dma_last_dim=4096)
             dma("P", "gd2", 32, y2, v("PP", 0, ROT), accum_op=Op.add, max_dma_last_dim=4096)
-            needs()
+            need1(); need2(); need3()
 
-    ts(v("YI"), v("KM", 1, 640, 2), 7, Op.logical_shift_right)
+    ts(v("YI"), v("KM", 1, 160, 2), 7, Op.logical_shift_right)
     ts(v("YT"), v("YI"), 8192.0, Op.is_ge, -8193.0, Op.mult)
     tt(v("YC"), v("YI"), v("YT"), Op.add)
-    dma("D", "out", 48, ext(T.yc[:], "yc"), v("YC"))
+    for q in range(4):
+        mm(v("KT", 80 * q, 80 * q + 80, 1, 8), w("SY", 8 * q, 8), v("YC"), True, True)
+    for q in range(4): do("V", g.vector.tensor_copy, (T.YO[:, q, :], [("YO", q, q + 1, 1)]), [v("KT", 80 * q, 80 * q + 80, 1, 8)], (T.KT[0:8, 80 * q:80 * q + 80],))
+    for t in range(RO): dma("D", "out", 112, ext(T.yc[:, 64 * t:64 * t + 64], "yc%d" % t), (T.YO[:, :, 16 * t:16 * t + 16], [("YO", 0, 4, 1)]))
     landed("l", RO, "LL", 8); landed("n", RO, "MM", 64)
     vc(w("YPo", 0, 4), w("LL", 44, 4))
     vc(w("YPo", 4, 4), w("LL", 40, 4))
     ts(v("YZo"), w("MM", 320, 64), -128.0, Op.add)
-    dma("D", "out", 48, ext(T.yp[:], "yp"), v("YPo"))
-    dma("D", "out", 48, ext(T.yz[:], "yz"), v("YZo"))
+    dma("D", "out", 112, ext(T.yp[:], "yp"), v("YPo"))
+    dma("D", "out", 112, ext(T.yz[:], "yz"), v("YZo"))
     wait("P", "ls", sent[0])
     wait("P", "gd2", 32)
-    wait("D", "out", 48)
+    wait("D", "out", 112)
     for q in "VSTP": wait("D", q, cnt[q])

from concourse.mybir import AluOpType as Op, AxisListType, ActivationFunctionType as Act

W, P, RO = 4096, 64, 5
ROT = 315
BAD = float(1 << 20)
BIG = float(1 << 27)
OUT = 16384.0
SCRATCH = {}


def _bufs(dtype, text, where="sbuf"):
    for item in text.split(","):
        f = item.split()
        SCRATCH[f[0]] = (where, [int(f[2]) if len(f) > 2 else 128, int(f[1])], dtype)


_bufs("bfloat16", "GF2 512, GP2 512, C2f 64 64, EXf 128 64, FA 4160, PP 4160, NA 4096, ND 64, MM 384, NS 320, NR 1024, GF 9216, GP 9216, AB 768, MN 768, ZER 64, YZo 64")
_bufs("bfloat16", "TBf 32, E8 512, LIDX 128 2, IDXR 512 2, INDF 64, INDP 64, IND1 64, DIAG 192, RS16 192, RS64 768, ONE 128 2, XPRE 256 1, JPRE 160 2, MPRE 192 1")
_bufs("int32", "RM 1536, CM 2048, PR 8, PI 1, QI 4, CI 192, TI 256, DI 12, GPi 1, SPi 1, MG 128, MS 192, M7 128, M1 128, MH 128 64, M8 64, Pc 608, Pi 608, KM 160, T32 32, PF 192, FI 192, YI 80")
_bufs("uint16", "LL 48, LS 40, OF 608, TNu 4, TS 12")
_bufs("float16", "C2p 64 64, EXp 128 64, IJ 768, IS 640, IJD 128, BLK 128, BLKo 128, SEL 2048, DUP 512, M2S 256, TMP 512, ID 128, I2 128, I2h 256, EI 128, EJ 128, SELW 128, SELJ 128, TRI 256, Xf 64, UAW 128, B01 64, VD 192")
_bufs("float32", "PRf 8, GPf 1, SPf 1, PIf 1, QP 4, SPQ 16, SPm 2, SY 32, cX 1, cW 1, cJ 1, ownA 1, ownB 1, ownT 1, RS2 32, DUM 12, Yp 64, YM 128, Y2 32, S1 32, ST 32, LD 128, LSc 128, UWs 128, SL 192, TN 4, DU 12, DV 12, DW 12, YT 80, YC 80, YPo 8")
_bufs("float32", "XB0 512, XB1 512, JI 512, MB 512, KT 512, TAB 512, UW 512, KEY 512", "psum")
SCRATCH["KEY"] = ("psum", [128, 8, 64], "float32")
SCRATCH["YO"] = ("sbuf", [8, 4, 80], "float32")
SEMAPHORES = ["sV", "sS", "sT", "sP", "ls", "out", "gd", "gd2"] + ["ld%d" % k for k in range(7)] + ["%s%d" % (m, t) for m in "lin" for t in range(1, RO + 1)]


def rank_program(g, core, T, topo):
    rank = T.rank_of(core)
    if rank is None:
        return
    n_ranks = len(T.cores)
    QS = {"V": g.vector, "S": g.scalar, "T": g.tensor, "P": g, "D": g.sync}
    cnt = {q: 0 for q in "VSTP"}
    known = {q: {} for q in QS}
    snaps = {}
    hist = {}

    def v(name, lo=0, hi=None, st=1, r=None):
        hi = SCRATCH[name][1][1] if hi is None else hi
        return T[name][0:(r or SCRATCH[name][1][0]), lo:hi:st], [(name, lo, hi, st)]
    def w(name, lo, n, st=1): return v(name, lo, lo + n * st, st)
    def ix(name, hi, lst): return T[name][:, 0:hi].indirect(lst[0]), [(name, 0, hi, 1)] + lst[1]
    def key(ap): return ap, [("KEY", 0, 512, 1)]
    def ext(ap, name=None): return ap, [(name, 0, 1, 1)] if name else []

    def wait(q, ev, n):
        if known[q].get(ev, 0) < n:
            QS[q].wait_ge(T.sem["s" + ev if ev in cnt else ev], n)
            known[q][ev] = n
            for e2, n2 in snaps.get((ev, n), {}).items(): known[q][e2] = max(known[q].get(e2, 0), n2)

    def order(q, rd, wr, ev, n):
        need = {}
        acc = [(x, False) for o in rd for x in o[1]] + [(x, True) for x in wr[1]]
        for (name, lo, hi, st), write in acc:
            bank = SCRATCH[name][0] == "psum" if name in SCRATCH else False
            for a in hist.get(name, []):
                apart = a[1] <= lo or hi <= a[0] or (a[2] == st > 1 and (a[0] - lo) % st)
                if bank and a[3] != q: apart = False
                elif not (write or a[5]) or (q == a[3] == "T"): continue
                if not apart: need[a[3]] = max(need.get(a[3], 0), a[4])
        for e, c in sorted(need.items(), key=lambda x: (x[0] == q, x[0])): wait(q, e, c)
        snaps[(ev, n)] = dict(known[q])
        for (name, lo, hi, st), write in acc:
            bank = SCRATCH[name][0] == "psum" if name in SCRATCH else False
            hist[name] = [a for a in hist.get(name, []) if not ((bank and a[3] != q) or (lo <= a[0] and a[1] <= hi and a[2] % st == 0 and (a[0] - lo) % st == 0 and (write or (a[3] == ev and not a[5]))))]
            hist[name].append([lo, hi, st, ev, n, write])

    def do(q, fn, out, ins, args, **kw):
        order(q, ins, out, q, cnt[q] + 1)
        cnt[q] += 1
        fn(out[0], *args, **kw).then_inc(T.sem["s" + q], 1)

    def dma(q, ev, n, out, in_, **kw):
        order(q, [in_], out, ev, n)
        QS[q].dma_start(out[0], in_[0], **kw).then_inc(T.sem[ev], 16)

    def vc(out, a): do("V", g.vector.tensor_copy, out, [a], (a[0],))
    def tt(out, a, b, op): do("V", g.vector.tensor_tensor, out, [a, b], (a[0], b[0], op))
    def ts(out, a, s1, op0, s2=None, op1=None):
        col = isinstance(s1, tuple)
        do("V", g.vector.tensor_scalar, out, [a, s1] if col else [a], (a[0], s1[0] if col else s1, s2, op0) + ((op1,) if op1 else ()))
    def scan(out, d0, d1, op0, op1): do("V", g.vector.tensor_tensor_scan, out, [d0, d1], (d0[0], d1[0], 0.0, op0, op1))
    def act(out, a, f=Act.Identity, bias=0.0, scale=1.0):
        col = isinstance(bias, tuple)
        do("S", g.scalar.activation, out, [a, bias] if col else [a], (a[0], f), bias=bias[0] if col else bias, scale=scale)
    def mm(out, l, r, st, sp): do("T", g.tensor.matmul, out, [l, r], (l[0], r[0], st, sp))
    def fill(out, c): do("V", g.vector.memset, out, [], (c,))
    def iota(name, pattern, base, cm, **kw): do("P", g.iota, v(name), [], (pattern, base, cm), **kw)

    sent = [0]

    def send(what, t, out, in_):
        dst = T.cores[(rank + 1 + t % 3) % n_ranks]
        eng = topo.engines(core, dst)[:8]
        sent[0] += len(eng)
        order("P", [in_], ext(None), "ls", sent[0])
        rid, pid, _ = topo.addr(dst)
        g.remote_dma(out[0], in_[0], T.sem["%s%d" % (what, t + 1)], T.sem.ls, pid, rid, sum(1 << e for e in eng))

    def landed(what, t, name, n):
        src = T.cores[(rank - 1 - (t - 1) % 3) % n_ranks]
        hist.setdefault(name, []).append([n * t, n * t + n, 1, "%s%d" % (what, t), len(topo.engines(src, core)[:8]), True])

    dma("D", "ld0", 16, w("PR", 0, 4), ext(T.pcol[:]))
    dma("D", "ld1", 16, w("PR", 4, 4), ext(T.prow[:]))
    dma("S", "ld4", 16, v("RM"), ext(T.rmate[:]))
    dma("D", "ld3", 16, v("CM"), ext(T.cmate[:]))
    dma("D", "ld2", 16, v("ND"), ext(T.need[:]))
    dma("D", "ld5", 16, v("FA", ROT, W), ext(T.fig[:, 0:W - ROT]))
    dma("D", "ld6", 16, v("FA", 0, ROT), ext(T.fig[:, W - ROT:W]))

    iota("PI", [[0, 1]], 0, 1)
    iota("CI", [[1, 192]], 0, 0)
    iota("QI", [[-32, 4]], 0, 1)
    fill(v("RS64"), BIG)
    iota("IDXR", [[0, 8], [1, 8], [8, 8]], 0, 64, allow_small_or_imprecise_dtypes=True)
    iota("TI", [[-16, 4], [1, 64]], 0, 0)
    iota("DI", [[0, 3], [16, 4]], W - 2048, 0)
    do("P", g.affine_select, v("RS64"), [v("RS64")], (T.RS64[:], [[0, 12], [1, 64]], Op.is_equal, 0.0, 0, 0))
    for name, c in (("ONE", 1.0), ("XPRE", 17.0), ("JPRE", 1.0), ("MPRE", -2048.0), ("ZER", 0.0), ("S1", 0.0)): fill(v(name), c)
    fill(v("JPRE", 0, 64, 1, 1), 16.0)
    fill(v("JPRE", 64, 160, 1, 1), 592.0)
    c128, SP, GP_, PI = v("CI", 0, 128), v("SPf"), v("GPf"), v("PIf")
    ts(v("SPi"), v("PI"), 15, Op.bitwise_and)
    ts(v("GPi"), v("PI"), 4, Op.logical_shift_right)
    ts(v("MG"), c128, 4, Op.logical_shift_right)
    ts(v("MS"), v("CI"), 15, Op.bitwise_and)
    vc(SP, v("SPi")); vc(GP_, v("GPi")); vc(PI, v("PI")); vc(v("QP"), v("QI"))
    ts(v("BLK"), v("MG"), GP_, Op.is_equal)
    ts(v("SPQ"), v("CI", 0, 16), SP, Op.is_equal, 2.0, Op.mult)
    ts(v("DIAG"), v("MS"), SP, Op.is_equal)
    ts(v("M7"), c128, 7, Op.bitwise_and)
    ts(v("M1"), c128, 1, Op.bitwise_and)
    for s in range(8): ts(w("SEL", 128 * s, 128), v("BLK"), w("SPQ", s, 1), Op.mult)
    ts(v("cX"), SP, 8.0, Op.is_ge, 100.0, Op.mult)
    ts(w("SPm", 1, 1), SP, -8.0, Op.add)
    tt(w("SPm", 0, 1), SP, v("cX"), Op.add)
    ts(v("ID"), c128, PI, Op.is_equal)
    ts(v("I2"), c128, PI, Op.is_equal, 2.0, Op.mult)
    ts(w("I2h", 0, 128), w("MS", 0, 128), 8.0, Op.is_lt)
    ts(w("I2h", 128, 128), w("MS", 0, 128), 8.0, Op.is_ge)
    for p in range(2):
        ts(w("TMP", 128 * p, 128), v("M7"), w("SPm", p, 1), Op.is_equal, 2.0, Op.mult)
        ts(w("TMP", 256 + 128 * p, 128), w("MS", 0, 128), w("SPm", p, 1), Op.is_equal)
        tt(w("TMP", 128 * p, 128), w("TMP", 128 * p, 128), v("BLK"), Op.mult)
        tt(w("M2S", 128 * p, 128), w("TMP", 256 + 128 * p, 128), v("BLK"), Op.mult)
        for h in range(2): tt(w("DUP", 256 * p + 128 * h, 128), w("TMP", 128 * p, 128), w("I2h", 128 * h, 128), Op.mult)
    for h in range(2): tt(w("I2h", 128 * h, 128), w("I2h", 128 * h, 128), v("I2"), Op.mult)
    for h, name in ((0, "EI"), (1, "EJ")):
        ts(w("TMP", 128 * h, 128), w("MS", 0, 128), 8.0 + h, Op.is_equal)
        tt(v(name), w("TMP", 128 * h, 128), v("ID"), Op.mult)
    ts(v("M8"), w("CI", 0, 64), 3, Op.logical_shift_right)
    ts(v("MH"), v("CI", 0, 128, 1, 64), 1, Op.logical_shift_right)
    p64 = v("PIf", 0, 1, 1, 64)
    ts(v("EXp"), v("MH"), p64, Op.is_equal, 64.0, Op.mult)
    ts(v("EXf"), v("MH"), p64, Op.is_equal, BAD, Op.mult)
    ts(v("INDF"), v("M8"), GP_, Op.is_equal, BAD, Op.mult)
    ts(v("INDP"), v("M8"), GP_, Op.is_equal, 64.0, Op.mult)
    ts(v("IND1"), v("M8"), GP_, Op.is_equal)
    ts(v("LIDX"), v("M1", 0, 128, 1, 2), v("PIf", 0, 1, 1, 2), Op.is_equal)
    vc(w("LL", 0, 8), v("PR"))
    vc(v("PRf"), v("PR"))
    for q in range(8): ts(w("IJD", 16 * q, 16), w("DIAG", 0, 16), w("PRf", q, 1), Op.mult)
    mm(w("UW", 0, 128), v("BLK"), v("IJD"), True, True)
    ts(w("MM", 0, 64), v("ND"), 128.0, Op.add)
    for q in range(4): ts(w("E8", 128 * q, 128), v("MG"), w("QP", q, 1), Op.is_equal)
    vc(w("IJ", 0, 128), w("UW", 0, 128))
    ts(v("RS16"), v("MS"), 0.0, Op.is_gt)
    ts(v("RS2"), w("M1", 0, 32), 0.0, Op.is_equal, BAD, Op.mult)
    ts(v("ownA"), SP, 8.0, Op.mult)
    ts(v("ownT"), SP, 8.0, Op.is_ge, 2 * BAD, Op.mult)
    ts(v("cW"), SP, 8.0, Op.is_le)
    tt(v("ownB"), SP, v("ownT"), Op.add)
    ts(v("cJ"), SP, 9.0, Op.is_equal)
    ts(v("ownB"), v("ownB"), BAD, Op.min)
    ts(v("SELW"), v("BLK"), v("cW"), Op.mult)
    ts(v("SELJ"), v("BLK"), v("cJ"), Op.mult)
    ts(v("BLKo"), v("BLK"), OUT / 16, Op.mult)

    def late_constants():
        ts(v("TRI"), v("TI"), SP, Op.is_ge, 32768.0, Op.mult)
        ts(v("DUM"), v("DI"), SP, Op.add)
        for s in range(8, 16): ts(w("SEL", 128 * s, 128), v("BLK"), w("SPQ", s, 1), Op.mult)
        for q in range(4): ts(w("SY", 8 * q, 8), v("CI", 0, 8), w("QP", q, 1), Op.is_equal)

    one1 = v("ONE", 0, 128, 1, 1)
    BANKS = ("XB0", "XB1", "KT")
    for t in range(RO):
        par, last = t % 2, t == RO - 1
        jw, iw = w("IJ", 128 * t, 64), w("IJ", 128 * t + 64, 64)
        need = w("MM", 64 * t, 64)
        if t:
            landed("l", t, "LL", 8); landed("i", t, "IJ", 128); landed("n", t, "MM", 64)

        for h in range(2): mm(w("XB%d" % h, 0, 256), one1, v("XPRE"), True, False)
        vc(v("Xf"), ix("CM", 2048, w("LL", 8 * t, 4)))
        ts(v("Yp"), ix("RM", 1536, w("LL", 8 * t + 4, 4)), 2.0, Op.mult, 593.0, Op.add)
        for b in range(8): mm(w("XB%d" % (b // 4), 64 * (b % 4), 64), w("SEL", 128 * (8 * par + b), 128), v("Xf"), False, b % 4 == 3)

        def prod(b): tt(w("Pc", 64 * b, 64), w("XB%d" % (b // 4), 64 * (b % 4), 64), v("Yp"), Op.mult)
        def shift(lo, hi): ts(v("Pi", lo, hi), v("Pc", lo, hi), 5, Op.logical_shift_right, W - 1, Op.bitwise_and)
        def conv(lo, hi): vc(v("OF", lo, hi), v("Pi", lo, hi))

        for b in range(4): prod(b)
        shift(0, 128)
        for b in range(4, 8): prod(b)
        conv(0, 128)
        shift(128, 512)
        conv(128, 512)
        mm(w("JI", 0, 160), v("ONE"), v("JPRE"), True, False)
        mm(w("KT", 0, 32), one1, v("XPRE", 0, 32), True, False)
        mm(key(T.KEY[:]), v("LIDX"), v("IDXR"), True, False)
        for h in range(2): mm(w("KT", 0, 32), w("DUP", 256 * par + 128 * h, 128), v("Xf", h, 64, 2), False, h == 1)
        mm(w("MB", 320, 64), w("M2S", 128 * par, 128), v("Xf"), True, False)
        mm(w("JI", 0, 64), v("I2"), iw, False, False)
        mm(w("JI", 64, 64), v("I2"), jw, False, False)
        for h in range(2): mm(w("JI", 128, 32), w("I2h", 128 * h, 128), v("IJ", 128 * t + h, 128 * t + 64, 2), False, h == 1)
        mm(w("MB", 320, 64), v("EI"), iw, False, False)
        mm(w("MB", 320, 64), v("EJ"), jw, False, True)
        for a in range(16): act(v("NR", a, 1024, 16), need, bias=-128.0)
        act(w("FA", W, P), need, scale=2.0, bias=-255.0)

        def pos(lo, hi):
            out, off = (v("GP2"), v("OF", 576, 608)) if lo == 9 else (v("GP", 1024 * lo, 1024 * hi), v("OF", 64 * lo, 64 * hi))
            act(out, ix("PP" if t else "FA", W, off), scale=1.0 if t else 2.0)
        def fails(b):
            if b == 9: tt(v("GF2"), ix("FA", W, v("OF", 576, 608)), v("NR", 0, 1024, 2), Op.is_lt)
            else: tt(w("GF", 1024 * b, 1024), ix("FA", W, w("OF", 64 * b, 64)), v("NR"), Op.is_lt)
        def keys(which):
            for b in which:
                for n, bank in (("P", "UW"), ("F", "TAB")):
                    for c in range(8):
                        if b < 8:
                            mm(key(T.KEY[:, :, 8 * b + c]), v("G" + n, 1024 * b + c, 1024 * b + 1024, 8), v("IND" + n, 0, 64, 8), False, (n, b, c) == ("F", 7, 7))
                        elif b == 8:
                            mm(key(T.KEY[:, :, c:64:8]), v("G" + n, 8192 + c, 9216, 8), v("IND" + n), False, False)
                        else:
                            mm(v(bank, 256 + c, 320, 8, 64), v("G" + n + "2", c, 512, 8), v("IND1", 0, 64, 8), True, True)

        pos(0, 1); pos(1, 2)
        act(v("Y2"), w("JI", 128, 32))
        fails(0); fails(1)
        tt(w("Pc", 512, 64), w("JI", 0, 64), v("Yp"), Op.mult)
        tt(w("Pc", 576, 32), w("KT", 0, 32), v("Y2"), Op.mult)
        shift(512, 608)
        conv(512, 608)
        pos(2, 3); pos(8, 9); pos(9, 10); pos(3, 5)
        for b in (2, 8, 9, 3): fails(b)
        keys((0, 1, 2, 8, 9, 3))
        act(v("C2f"), v("TAB", 256, 320, 1, 64))
        vc(v("C2p"), v("UW", 256, 320, 1, 64))
        pos(5, 7); pos(7, 8)
        for b in (4, 5, 6, 7): fails(b)
        for c in range(8):
            mm(key(T.KEY[:, :, c:64:8]), v("EXp"), v("C2p"), False, False)
            mm(key(T.KEY[:, :, c:64:8]), v("EXf"), v("C2f"), False, False)
        keys((4, 5, 6, 7))
        act(w("YM", 0, 64), v("Yp"), bias=-296.5, scale=0.5)
        act(w("YM", 64, 64), w("MB", 320, 64))
        mm(w("MB", 0, 192), one1, v("MPRE"), True, False)
        if t == 0: act(v("PP", 0, W), v("FA", 0, W), scale=2.0)

        for k in range(8): do("V", g.vector.tensor_reduce, w("S1", k, 1), [key(None)], (T.KEY[:, k, :], AxisListType.X, Op.min))
        do("V", g.vector.transpose, v("ST"), [v("S1")], (T.S1[:],))
        scan(w("KM", 32 * t, 32), v("RS2"), v("ST"), Op.max, Op.min)
        km = v("KM", 32 * t + 1, 32 * t + 32, 2)
        ts(v("T32", 0, 32, 2), km, 0x7FF00078, Op.bitwise_and)
        ts(v("T32", 1, 32, 2), km, 0x7FF00007, Op.bitwise_and)
        vc(v("TBf"), v("T32"))
        for q in range(4): mm(w("TAB", 32 * q, 32), w("E8", 128 * q, 128), v("TBf"), True, True)
        ts(w("KT", 256, 64), v("TAB", 0, 128, 2), v("ownA"), Op.is_equal)
        ts(w("KT", 320, 64), v("TAB", 1, 128, 2), v("ownB"), Op.is_equal)
        ts(v("B01"), v("TAB", 1, 128, 2), BAD, Op.is_ge)
        tt(v("UAW"), w("KT", 256, 128), v("YM"), Op.mult)
        def names(bank, o):
            mm(w(bank, o, 64), v("BLK"), w("UAW", 0, 64), True, False)
            mm(w(bank, o, 64), v("SELJ"), w("UAW", 64, 64), False, True)
            mm(w(bank, o + 64, 64), v("SELW"), w("UAW", 64, 64), True, True)
        names("UW", 0)
        for k in range(3): mm(w("MB", 64 * k, 64), v("BLKo"), v("B01"), False, k == 2)
        names("MB", 192)
        if t == 0: late_constants()
        for bank in BANKS: mm(w(bank, 0, 256), v("ID"), v("TRI"), True, False)
        tt(v("LD"), w("UW", 0, 128), w("DIAG", 0, 128), Op.mult)
        scan(v("LSc"), w("RS16", 0, 128), v("LD"), Op.mult, Op.add)
        vc(w("LS", 8 * t, 8), v("LSc", 15, 128, 16))
        send("l", t, w("LL", 8 * t + 8, 8), w("LS", 8 * t, 8))

        act(w("UWs", 0, 64), w("MB", 192, 64), scale=2.0, bias=593.0)
        act(w("UWs", 64, 64), w("MB", 256, 64), scale=2.0, bias=17.0)
        def f_col(k): ts(w("FI", 64 * k, 64), w("PF", 64 * k, 64), 5, Op.logical_shift_right, W - 1, Op.bitwise_and)
        def f_out(k): tt(w("TAB", 192 + 64 * k, 64), w("FI", 64 * k, 64), w("MB", 64 * k, 64), Op.add)
        def f_own(k): tt(w("VD", 64 * k, 64), w("TAB", 192 + 64 * k, 64), w("DIAG", 0, 64), Op.mult)
        def f_list(k): scan(w("SL", 64 * k, 64), w("RS16", 0, 64), w("VD", 64 * k, 64), Op.mult, Op.add)

        def compare(k):
            for q in range(4): mm(w(BANKS[k], 64 * q, 64), v("BLK"), w("VD", 64 * k, 64), False, q == 3)
            for q in range(4):
                c = 4 * k + q
                act(w("AB", 64 * c, 64), w(BANKS[k], 64 * q, 64), Act.Abs, scale=-1.0, bias=w("SL", 16 * c + 15, 1))

        def need1(): tt(v("TN"), v("SL", 15, 64, 16), w("DUM", 0, 4), Op.min)
        def need2(): ts(v("TNu"), v("TN"), 2048.0, Op.add)
        def need3():
            ts(w("NS", 64 * t, 64), ix("FA", W + P, v("TNu")), 0.5, Op.mult, 127.75, Op.add)
            send("n", t, w("MM", 64 * t + 64, 64), w("NS", 64 * t, 64))

        tt(w("PF", 0, 64), w("UWs", 0, 64), w("UWs", 64, 64), Op.mult)
        tt(w("PF", 64, 128), v("UWs"), w("JI", 0, 128), Op.mult)
        f_col(0); f_col(1); f_out(0); f_col(2); f_own(0); f_out(1); f_list(0); f_own(1)
        compare(0)
        if not last: need1()
        f_list(1)
        compare(1)
        if not last: need2()
        f_out(2)
        if not last: need3()
        f_own(2); f_list(2)
        compare(2)

        if not last:
            vc(w("IS", 128 * t, 128), w("UW", 0, 128))
            send("i", t, w("IJ", 128 * t + 128, 128), w("IS", 128 * t, 128))
            act(w("NA", 1024 * t, 1024), w("FA", 1024 * t, 1024), scale=-1.0)
        for lo, n in ((0, 512), (512, 256)): scan(w("MN", lo, n), w("RS64", lo, n), w("AB", lo, n), Op.max, Op.min)
        ts(v("DU"), v("MN", 63, 768, 64), 0.0, Op.is_equal, OUT, Op.mult)
        tt(v("DV"), v("DU"), v("SL", 15, 192, 16), Op.add)
        tt(v("DW"), v("DV"), v("DUM"), Op.min)
        ts(v("TS"), v("DW"), 2048.0, Op.add)
        for k in range(3): vc(ix("PP", W + P, w("TS", 4 * k, 4)), v("ZER"))
        y1, y2 = ext(T.yf[:, 0:W - ROT], "yf1"), ext(T.yf[:, W - ROT:W], "yf2")
        if t == RO - 2:
            dma("P", "gd", 32, y1, v("NA", ROT, W))
            dma("P", "gd", 32, y2, v("NA", 0, ROT))
        if last:
            dma("P", "gd2", 32, y1, v("PP", ROT, W), accum_op=Op.add, max_dma_last_dim=4096)
            dma("P", "gd2", 32, y2, v("PP", 0, ROT), accum_op=Op.add, max_dma_last_dim=4096)
            need1(); need2(); need3()

    ts(v("YI"), v("KM", 1, 160, 2), 7, Op.logical_shift_right)
    ts(v("YT"), v("YI"), 8192.0, Op.is_ge, -8193.0, Op.mult)
    tt(v("YC"), v("YI"), v("YT"), Op.add)
    for q in range(4):
        mm(v("KT", 80 * q, 80 * q + 80, 1, 8), w("SY", 8 * q, 8), v("YC"), True, True)
    for q in range(4): do("V", g.vector.tensor_copy, (T.YO[:, q, :], [("YO", q, q + 1, 1)]), [v("KT", 80 * q, 80 * q + 80, 1, 8)], (T.KT[0:8, 80 * q:80 * q + 80],))
    for t in range(RO): dma("D", "out", 112, ext(T.yc[:, 64 * t:64 * t + 64], "yc%d" % t), (T.YO[:, :, 16 * t:16 * t + 16], [("YO", 0, 4, 1)]))
    landed("l", RO, "LL", 8); landed("n", RO, "MM", 64)
    vc(w("YPo", 0, 4), w("LL", 44, 4))
    vc(w("YPo", 4, 4), w("LL", 40, 4))
    ts(v("YZo"), w("MM", 320, 64), -128.0, Op.add)
    dma("D", "out", 112, ext(T.yp[:], "yp"), v("YPo"))
    dma("D", "out", 112, ext(T.yz[:], "yz"), v("YZo"))
    wait("P", "ls", sent[0])
    wait("P", "gd2", 32)
    wait("D", "out", 112)
    for q in "VSTP": wait("D", q, cnt[q])
